import numpy as np
import ml_dtypes


def mxq(x, axis, fmt="e4m3"):
    dtype, down = {"e4m3": (ml_dtypes.float8_e4m3fn, 7), "e5m2": (ml_dtypes.float8_e5m2, 14)}[fmt]
    v = np.moveaxis(np.asarray(x, np.float32).astype(ml_dtypes.bfloat16).astype(np.float64), axis, -1)
    blocks = v.reshape(v.shape[:-1] + (-1, 32))
    amax = np.abs(blocks).max(-1, keepdims=True)
    byte = np.maximum(np.where(amax > 0, np.frexp(amax)[1] - 1 + 127, 0) - down, 1)
    scale = np.exp2(byte - 127.0)
    codes = (blocks / scale).astype(np.float32).astype(dtype).astype(np.float64)
    return np.moveaxis((codes * scale).reshape(v.shape), -1, axis)


WIDE = False


def mx_kscale(k):
    if not WIDE:
        return np.ones(k)
    levels = np.array([10, -10, 5, -5, 0])
    if k % 512:
        return np.exp2(np.random.permutation(np.resize(levels, k // 32))).repeat(32)
    a = np.empty((k // 512, 16))
    for p in range(k // 512):
        a[p, :8] = np.random.permutation(np.resize(levels, 8))
        for g in range(8):
            far = levels[np.abs(levels - a[p, g]) >= 10]
            a[p, g + 8] = far[np.random.randint(len(far))]
    return np.exp2(a.ravel()).repeat(32)


def f64(x):
    return np.asarray(x).astype(np.float64)


def striped(idx):
    return np.tile(idx.reshape(-1, 16).T, (8, 1)).astype(np.uint16)


def unstriped(offs):
    return offs[:16].T.reshape(-1).astype(np.int64)


E2M1 = np.array([0.0, 0.5, 1.0, 1.5, 2.0, 3.0, 4.0, 6.0, -0.0, -0.5, -1.0, -1.5, -2.0, -3.0, -4.0, -6.0])


def pack_weight(w, fmt):
    k, n = w.shape
    w = f64(np.asarray(w, np.float32).astype(ml_dtypes.bfloat16)).reshape(k // 32, 32, n)
    amax = np.abs(w).max(1)
    if fmt == "e4m3":
        byte = np.frexp(amax)[1] - 1 + 127 - 7
    else:
        mant, ex = np.frexp(amax / 6.0)
        byte = np.where(mant > 0.5, ex, ex - 1) + 127
    byte = np.clip(np.where(amax > 0, byte, 1), 1, 254)
    scaled = (w * np.exp2(127.0 - byte)[:, None, :]).reshape(k, n).astype(np.float32)
    by_word = np.ascontiguousarray(scaled.reshape(k // 512, 128, 4, n).transpose(0, 1, 3, 2))
    if fmt == "e4m3":
        words = by_word.astype(ml_dtypes.float8_e4m3fn).view(np.uint8)
    else:
        c = by_word.astype(ml_dtypes.float4_e2m1fn).view(np.uint8) & 0xF
        words = (c[..., 0::2] | (c[..., 1::2] << 4)).reshape(k // 512, 128, 2 * n)
    return np.ascontiguousarray(words), np.ascontiguousarray(byte.astype(np.uint8).reshape(k // 512, 16, n))


def unpack_weight(words, scales, fmt):
    g, _, n = scales.shape
    words = np.ascontiguousarray(words).reshape(g, 128, n, -1)
    if fmt == "e4m3":
        vals = words.view(ml_dtypes.float8_e4m3fn).astype(np.float64)
    else:
        nib = np.empty((g, 128, n, 4), np.uint8)
        nib[..., 0::2] = words & 0xF
        nib[..., 1::2] = words >> 4
        vals = E2M1[nib]
    vals = vals * np.repeat(np.exp2(scales.astype(np.float64) - 127.0), 8, axis=1)[..., None]
    return vals.transpose(0, 1, 3, 2).reshape(g * 512, n)


def gelu(v):
    return 0.5 * v * (1.0 + np.tanh(np.sqrt(2.0 / np.pi) * (v + 0.044715 * v**3)))


K, H, N, T, S, P = 1024, 1024, 768, 4096, 1024, 512

def setup_inputs():
    n = np.random.standard_normal
    s = mx_kscale(K)[:, None]
    u = mx_kscale(H)[:, None]
    tab_words, tab_scales = pack_weight(n((K, T)) * s, "e4m3")
    wn = (1.5 * n((K, H)) / np.sqrt(K) / s).astype(np.float32)
    wd_words, wd_scales = pack_weight(1.5 * n((K, H)) / np.sqrt(K) / s, "e2m1")
    wa_words, wa_scales = pack_weight(n((H, N)) / np.sqrt(H) / u, "e2m1")
    wb = (n((H, N)) / np.sqrt(H) / u).astype(np.float32)
    return {
        "tab_words": tab_words, "tab_scales": tab_scales,
        "offs": striped(np.random.permutation(T)[:S]),
        "pos1": striped(np.random.permutation(S)[:P]),
        "pos2": striped(np.random.permutation(S)[:P]),
        "wn": wn,
        "wd_words": wd_words, "wd_scales": wd_scales,
        "gain": (np.exp(0.4 * n(H)) * u[:, 0]).astype(np.float32),
        "va": (0.6 * n(H) * u[:, 0]).astype(np.float32),
        "vb": (0.5 * n(H) * u[:, 0]).astype(np.float32),
        "wa_words": wa_words, "wa_scales": wa_scales,
        "wb": wb,
    }

def reference(tab_words, tab_scales, offs, pos1, pos2, wn, wd_words, wd_scales, gain, va, vb, wa_words, wa_scales, wb):
    v = unpack_weight(tab_words, tab_scales, "e4m3")[:, unstriped(offs)]
    num = mxq(f64(wn), 0, "e4m3").T @ v
    den = unpack_weight(wd_words, wd_scales, "e2m1").T @ v
    h = num / (1.0 + np.abs(den)) * f64(gain)[:, None]
    xa = h[:, unstriped(pos1)] + f64(va)[:, None]
    xb = np.maximum(h[:, unstriped(pos2)], f64(vb)[:, None])
    ya = unpack_weight(wa_words, wa_scales, "e2m1").T @ mxq(xa, 0, "e4m3")
    yb = mxq(f64(wb), 0, "e4m3").T @ mxq(xb, 0, "e4m3")
    return np.minimum(ya, yb)

@@ -1,0 +1,296 @@
+from contextlib import ExitStack
+
+import concourse.mybir as mybir
+
+K, H, N, T, S, PICK = 1024, 1024, 768, 4096, 1024, 512
+FLOPS = 2 * (2 * K * H * S + 2 * H * N * PICK)
+
+F32 = mybir.dt.float32
+BF16 = mybir.dt.bfloat16
+I32 = mybir.dt.int32
+U32 = mybir.dt.uint32
+U16 = mybir.dt.uint16
+U8 = mybir.dt.uint8
+FP8X4 = mybir.dt.float8_e4m3fn_x4
+FP4X4 = mybir.dt.float4_e2m1fn_x4
+ALU = mybir.AluOpType
+ACT = mybir.ActivationFunctionType
+
+P = 128
+PACK = 4
+PASS = P * PACK
+BANK = 512
+ALIGN = 64
+
+
+def tile_list_newborn_screen_features_kernel(
+    tc, tab_words, tab_scales, offs, pos1, pos2, wn, wd_words, wd_scales, gain, va, vb, wa_words, wa_scales, wb, out
+):
+    nc = tc.nc
+    with ExitStack() as ctx:
+        lists = ctx.enter_context(tc.tile_pool(name="lists", bufs=1))
+        keep = ctx.enter_context(tc.tile_pool(name="keep", bufs=1))
+        psum = ctx.enter_context(tc.psum_pool(name="psum", bufs=4))
+
+        def sbuf(name, shape, dtype, tag=None, bufs=1):
+            return keep.tile(shape, dtype, name=name, tag=tag or name, bufs=bufs, align_bytes=ALIGN)
+
+        def load_scale_rows(engines, plane, scales):
+            for q, engine in enumerate(engines):
+                engine.dma_start(
+                    out=plane[32 * q : 32 * q + 4, :, :].bitcast(I32),
+                    in_=scales[:, 4 * q : 4 * q + 4, :].rearrange("a r c -> r a c").bitcast(I32),
+                )
+
+        def zero(engine, plane):
+            engine.memset(plane[:].rearrange("p a c -> p (a c)").bitcast(I32), 0)
+
+        offs_t = lists.tile([P, S // 16], U16, name="offs_t")
+        pos1_t = lists.tile([P, PICK // 16], U16, name="pos1_t")
+        pos2_t = lists.tile([P, PICK // 16], U16, name="pos2_t")
+        nc.sync.dma_start(offs_t[:], offs)
+        nc.sync.dma_start(pos1_t[:], pos1)
+        nc.sync.dma_start(pos2_t[:], pos2)
+
+        def load_channel_vector(name, vec):
+            col = sbuf(name, [P, 2 * PACK], F32)
+            nc.scalar.dma_start(
+                out=col[:].rearrange("p (b t) -> p b t", b=2), in_=vec.rearrange("(b p t) -> p b t", b=2, t=PACK)
+            )
+            return col
+
+        va_col = load_channel_vector("va_col", va)
+        gain_col = load_channel_vector("gain_col", gain)
+        vb_col = load_channel_vector("vb_col", vb)
+
+        wd_sc_raw = sbuf("wd_sc_raw", [P, 2, H], U8, tag="stage_c")
+        zero(nc.vector, wd_sc_raw)
+        load_scale_rows([nc.gpsimd] + 3 * [nc.scalar], wd_sc_raw, wd_scales)
+        tab_sc = sbuf("tab_sc", [P, 2, T], U8, tag="stage_d")
+        zero(nc.vector, tab_sc)
+        load_scale_rows(4 * [nc.scalar], tab_sc, tab_scales)
+
+        wd_raw = sbuf("wd_raw", [P, 2, 2 * H], U8, tag="stage_a")
+        nc.sync.dma_start(out=wd_raw[:].bitcast(I32), in_=wd_words.rearrange("a p c -> p a c").bitcast(I32))
+
+        def load_tab(a, tag):
+            words = sbuf("tab_w%d" % a, [P, T], U32, tag=tag)
+            nc.sync.dma_start(out=words[:].bitcast(I32), in_=tab_words[a].rearrange("p t i -> p (t i)").bitcast(I32))
+            return words
+
+        def load_wn(a, b, tag):
+            raw = sbuf("wn_raw%d%d" % (a, b), [P, PACK, PASS], F32, tag=tag)
+            rows = wn[a * PASS : (a + 1) * PASS, b * PASS : (b + 1) * PASS]
+            nc.sync.dma_start(out=raw[:], in_=rows.rearrange("(p j) c -> p j c", j=PACK))
+            return raw
+
+        tab_w0 = load_tab(0, "stage_b")
+
+        va_rows = []
+        for b in range(2):
+            rows = sbuf("va_rows%d" % b, [P, PACK, PICK], F32, tag="slab_%s" % "ab"[b])
+            for t in range(PACK):
+                c = PACK * b + t
+                nc.scalar.copy(out=rows[:, t, :], in_=va_col[:, c : c + 1].to_broadcast([P, PICK]))
+            va_rows.append(rows)
+
+        wd_w = sbuf("wd_w", [P, 2, 2, PACK, 2 * P], U8)
+        nc.vector.tensor_copy(
+            out=wd_w[:].rearrange("p a b t (m e) -> p (a b) m t e", e=2),
+            in_=wd_raw[:].rearrange("p a (b m t e) -> p (a b) m t e", b=2, t=PACK, e=2),
+        )
+        tab_w1 = load_tab(1, "stage_a")
+        v_s = [sbuf("v_s%d" % a, [P, S], U8) for a in range(2)]
+        v_w = [[sbuf("v_w%d%d" % (a, f), [P, BANK], U32) for f in range(2)] for a in range(2)]
+
+        def gather_words(a, words):
+            for f in range(2):
+                nc.vector.tensor_copy(v_w[a][f][:], words[:].indirect(offs_t[:, 32 * f : 32 * (f + 1)]))
+
+        nc.vector.tensor_copy(v_s[0][:], tab_sc[:, 0, :].indirect(offs_t[:]))
+        wd_s = sbuf("wd_s", [P, 2, 2, PACK, P], U8)
+        nc.vector.tensor_copy(
+            out=wd_s[:].rearrange("p a b t m -> p (a b) m t"),
+            in_=wd_sc_raw[:].rearrange("p a (b m t) -> p (a b) m t", b=2, t=PACK),
+        )
+        wn_raw = {(0, 0): load_wn(0, 0, "stage_c")}
+        gather_words(0, tab_w0)
+        wn_raw[1, 0] = load_wn(1, 0, "stage_b")
+        nc.vector.tensor_copy(v_s[1][:], tab_sc[:, 1, :].indirect(offs_t[:]))
+        wn_raw[0, 1] = load_wn(0, 1, "stage_d")
+        gather_words(1, tab_w1)
+        wn_raw[1, 1] = load_wn(1, 1, "stage_a")
+
+        def quantise(name, woven, width):
+            codes = sbuf(name + "_w", [P, width], U32)
+            scales = sbuf(name + "_s", [P, width], U8)
+            nc.vector.quantize_mx(out=codes[:].bitcast(FP8X4), scales=scales[:], in_=woven[:])
+            return codes, scales
+
+        def weave_wn(copy, a, b):
+            woven = sbuf("wn_woven%d%d" % (a, b), [P, PACK * PASS], BF16, tag="woven", bufs=4)
+            copy(
+                woven[:].rearrange("p (t m j) -> p m j t", t=PACK, j=PACK),
+                wn_raw[a, b][:].rearrange("p j (m t) -> p m j t", t=PACK),
+            )
+            return woven
+
+        def weave(copy, name, planes, width):
+            woven = sbuf(name + "_woven", [P, PACK * width], BF16, tag="woven", bufs=4)
+            copy(
+                woven[:].rearrange("p (c i t) -> p c t i", i=4, t=PACK),
+                planes.rearrange("p t (c i) -> p c t i", i=4),
+            )
+            return woven
+
+        wn_mx = {}
+        for a in range(2):
+            wn_mx[a, 0] = quantise("wn%d0" % a, weave_wn(nc.vector.tensor_copy, a, 0), PASS)
+
+        wb_raw = []
+        for a in range(2):
+            raw = sbuf("wb_raw%d" % a, [P, PACK, N], F32, tag="stage_%s" % "cb"[a])
+            nc.sync.dma_start(out=raw[:], in_=wb[a * PASS : (a + 1) * PASS, :].rearrange("(p j) n -> p j n", j=PACK))
+            wb_raw.append(raw)
+
+        def damping(c):
+            b, t = divmod(c, PACK)
+            damp = sbuf("damp%d" % c, [P, S], F32, tag="damp", bufs=8)
+            halves = [damp[:, f * BANK : (f + 1) * BANK] for f in range(2)]
+            for f in range(2):
+                den = psum.tile([P, BANK], F32, name="den%d%d" % (c, f), tag="left")
+                for a in range(2):
+                    nc.tensor.matmul_mx(
+                        out=den[:],
+                        lhsT=wd_w[:, a, b, t, :].bitcast(FP4X4),
+                        lhsT_scale=wd_s[:, a, b, t, :],
+                        rhs=v_w[a][f][:].bitcast(FP8X4),
+                        rhs_scale=v_s[a][:, f * BANK : (f + 1) * BANK],
+                        start=(a == 0),
+                        stop=(a == 1),
+                    )
+                nc.scalar.activation(out=halves[f], in_=den[:], func=ACT.Abs)
+            for half in halves:
+                nc.scalar.activation(out=half, in_=half, func=ACT.Abs_reciprocal_sqrt, bias=1.0)
+            for half in halves:
+                nc.scalar.activation(out=half, in_=half, func=ACT.Square)
+            return damp
+
+        def features(c, damp):
+            b, t = divmod(c, PACK)
+            h = sbuf("h%d" % c, [P, S], F32, tag="h", bufs=6)
+            for f in range(2):
+                cols = slice(f * BANK, (f + 1) * BANK)
+                num = psum.tile([P, BANK], F32, name="num%d%d" % (c, f), tag="right")
+                for a in range(2):
+                    codes, scales = wn_mx[a, b]
+                    nc.tensor.matmul_mx(
+                        out=num[:],
+                        lhsT=codes[:, t * P : (t + 1) * P].bitcast(FP8X4),
+                        lhsT_scale=scales[:, t * P : (t + 1) * P],
+                        rhs=v_w[a][f][:].bitcast(FP8X4),
+                        rhs_scale=v_s[a][:, cols],
+                        start=(a == 0),
+                        stop=(a == 1),
+                    )
+                nc.vector.scalar_tensor_tensor(
+                    out=h[:, cols], in0=num[:], scalar=gain_col[:, c : c + 1], in1=damp[:, cols], op0=ALU.mult, op1=ALU.mult
+                )
+            return h
+
+        def pick_a(dst, h, c):
+            b, t = divmod(c, PACK)
+            nc.vector.tensor_tensor(dst[:, t, :], h[:].indirect(pos1_t[:]), va_rows[b][:, t, :], ALU.add)
+
+        def pick_b(dst, h, c, offsets):
+            nc.vector.tensor_copy(dst, h[:].indirect(offsets))
+            nc.vector.tensor_scalar(out=dst, in0=dst, scalar1=vb_col[:, c : c + 1], scalar2=None, op0=ALU.max)
+
+        HALF = PICK // 2
+        xa_f32 = [sbuf("xa_f32_0", [P, PACK, PICK], F32, tag="slab_d")]
+        xb0_f32 = sbuf("xb0_f32", [P, PACK, PICK], F32)
+        xb10_f32 = sbuf("xb10_f32", [P, PACK, HALF], F32)
+        damps = [damping(0), damping(1)]
+        hs = []
+        wn_woven = {}
+        wb_mx = {}
+
+        def quantise_wb(a, g):
+            name = "wb%d%d" % (a, g)
+            planes = wb_raw[a][:, :, g * (N // 2) : (g + 1) * (N // 2)]
+            wb_mx[a, g] = quantise(name, weave(nc.scalar.copy, name, planes, N // 2), N // 2)
+
+        for c in range(2 * PACK):
+            b, t = divmod(c, PACK)
+            if c + 2 < 2 * PACK:
+                damps.append(damping(c + 2))
+            if c < 2:
+                wn_mx[c, 1] = quantise("wn%d1" % c, weave_wn(nc.scalar.copy, c, 1), PASS)
+            elif c < 6:
+                quantise_wb(*divmod(c - 2, 2))
+            if c == PACK:
+                xa_f32.append(sbuf("xa_f32_1", [P, PACK, PICK], F32, tag="slab_a"))
+            hs.append(features(c, damps[c]))
+            pick_a(xa_f32[b], hs[c], c)
+            if b == 0:
+                pick_b(xb0_f32[:, t, :], hs[c], c, pos2_t[:])
+            else:
+                pick_b(xb10_f32[:, t, :], hs[c], c, pos2_t[:, 0:16])
+            if c == PACK - 1:
+                xa_mx = [quantise("xa0", weave(nc.vector.tensor_copy, "xa0", xa_f32[0][:], PICK), PICK)]
+                xb0_mx = quantise("xb0", weave(nc.vector.tensor_copy, "xb0", xb0_f32[:], PICK), PICK)
+
+        wa_w = sbuf("wa_w", [P, 2, 2 * N], U8, tag="stage_d")
+        nc.sync.dma_start(out=wa_w[:].bitcast(I32), in_=wa_words.rearrange("a p c -> p a c").bitcast(I32))
+        wa_s = sbuf("wa_s", [P, 2, N], U8, tag="stage_a")
+        zero(nc.vector, wa_s)
+        load_scale_rows(4 * [nc.sync], wa_s, wa_scales)
+        xa_mx.append(quantise("xa1", weave(nc.scalar.copy, "xa1", xa_f32[1][:], PICK), PICK))
+        xb1_mx = [quantise("xb10", weave(nc.scalar.copy, "xb10", xb10_f32[:], HALF), HALF)]
+        xb11_f32 = sbuf("xb11_f32", [P, PACK, HALF], F32, tag="slab_b")
+        for t in range(PACK):
+            pick_b(xb11_f32[:, t, :], hs[PACK + t], PACK + t, pos2_t[:, 16:32])
+        xb1_mx.append(quantise("xb11", weave(nc.vector.tensor_copy, "xb11", xb11_f32[:], HALF), HALF))
+
+        ya_sb = []
+        for pair in range(N // (2 * P)):
+            ya = sbuf("ya%d" % pair, [P, 2, PICK], F32, tag="damp", bufs=8)
+            for i in range(2):
+                n = 2 * pair + i
+                acc = psum.tile([P, PICK], F32, name="ya_acc%d" % n, tag="left")
+                for a in range(2):
+                    codes, scales = xa_mx[a]
+                    nc.tensor.matmul_mx(
+                        out=acc[:],
+                        lhsT=wa_w[:, a, 2 * n * P : 2 * (n + 1) * P].bitcast(FP4X4),
+                        lhsT_scale=wa_s[:, a, n * P : (n + 1) * P],
+                        rhs=codes[:].bitcast(FP8X4),
+                        rhs_scale=scales[:],
+                        start=(a == 0),
+                        stop=(a == 1),
+                    )
+                nc.scalar.copy(out=ya[:, i, :], in_=acc[:])
+            ya_sb.append(ya)
+
+        out_rows = out.rearrange("(g p) j -> p g j", p=P)
+        for f in range(2):
+            cols = slice(f * HALF, (f + 1) * HALF)
+            moving = [(xb0_mx[0][:, cols], xb0_mx[1][:, cols]), (xb1_mx[f][0][:], xb1_mx[f][1][:])]
+            for pair in range(N // (2 * P)):
+                acc = psum.tile([P, 2, HALF], F32, name="yb_acc%d%d" % (f, pair), tag="right")
+                for i in range(2):
+                    g, n = divmod(2 * pair + i, N // (2 * P))
+                    for a in range(2):
+                        codes, scales = wb_mx[a, g]
+                        nc.tensor.matmul_mx(
+                            out=acc[:, i, :],
+                            lhsT=codes[:, n * P : (n + 1) * P].bitcast(FP8X4),
+                            lhsT_scale=scales[:, n * P : (n + 1) * P],
+                            rhs=moving[a][0].bitcast(FP8X4),
+                            rhs_scale=moving[a][1],
+                            start=(a == 0),
+                            stop=(a == 1),
+                        )
+                result = ya_sb[pair][:, :, cols]
+                nc.vector.tensor_tensor(out=result, in0=acc[:], in1=result, op=ALU.min)
+                nc.sync.dma_start(out=out_rows[:, 2 * pair : 2 * pair + 2, cols], in_=result)

@@ -52,9 +52,20 @@ def tile_list_newborn_screen_features_kernel(
         nc.sync.dma_start(pos1_t[:], pos1)
         nc.sync.dma_start(pos2_t[:], pos2)
 
+        tab_sc = sbuf("tab_sc", [P, T], U8, tag="stage_d")
+        nc.vector.memset(tab_sc[:].bitcast(I32), 0)
+        for q in range(4):
+            nc.scalar.dma_start(
+                out=tab_sc[32 * q : 32 * q + 8, :].bitcast(I32), in_=tab_scales[:, 4 * q : 4 * q + 4, :].bitcast(I32)
+            )
+
+        wd_sc_raw = sbuf("wd_sc_raw", [P, 2, H], U8, tag="stage_c")
+        zero(nc.vector, wd_sc_raw)
+        load_scale_rows(2 * [nc.gpsimd] + 2 * [nc.scalar], wd_sc_raw, wd_scales)
+
         def load_channel_vector(name, vec):
             col = sbuf(name, [P, 2 * PACK], F32)
-            nc.scalar.dma_start(
+            nc.gpsimd.dma_start(
                 out=col[:].rearrange("p (b t) -> p b t", b=2), in_=vec.rearrange("(b p t) -> p b t", b=2, t=PACK)
             )
             return col
@@ -62,13 +73,6 @@ def tile_list_newborn_screen_features_kernel(
         va_col = load_channel_vector("va_col", va)
         gain_col = load_channel_vector("gain_col", gain)
         vb_col = load_channel_vector("vb_col", vb)
-
-        wd_sc_raw = sbuf("wd_sc_raw", [P, 2, H], U8, tag="stage_c")
-        zero(nc.vector, wd_sc_raw)
-        load_scale_rows([nc.gpsimd] + 3 * [nc.scalar], wd_sc_raw, wd_scales)
-        tab_sc = sbuf("tab_sc", [P, 2, T], U8, tag="stage_d")
-        zero(nc.vector, tab_sc)
-        load_scale_rows(4 * [nc.scalar], tab_sc, tab_scales)
 
         wd_raw = sbuf("wd_raw", [P, 2, 2 * H], U8, tag="stage_a")
         nc.sync.dma_start(out=wd_raw[:].bitcast(I32), in_=wd_words.rearrange("a p c -> p a c").bitcast(I32))
@@ -96,30 +100,31 @@ def tile_list_newborn_screen_features_kernel(
 
         wd_w = sbuf("wd_w", [P, 2, 2, PACK, 2 * P], U8)
         nc.vector.tensor_copy(
-            out=wd_w[:].rearrange("p a b t (m e) -> p (a b) m t e", e=2),
-            in_=wd_raw[:].rearrange("p a (b m t e) -> p (a b) m t e", b=2, t=PACK, e=2),
+            out=wd_w[:].bitcast(U16).rearrange("p a b t m -> p (a b) t m"),
+            in_=wd_raw[:].bitcast(U16).rearrange("p a (b m t) -> p (a b) t m", b=2, t=PACK),
         )
         tab_w1 = load_tab(1, "stage_a")
         v_s = [sbuf("v_s%d" % a, [P, S], U8) for a in range(2)]
-        v_w = [[sbuf("v_w%d%d" % (a, f), [P, BANK], U32) for f in range(2)] for a in range(2)]
-
-        def gather_words(a, words):
-            for f in range(2):
-                nc.vector.tensor_copy(v_w[a][f][:], words[:].indirect(offs_t[:, 32 * f : 32 * (f + 1)]))
-
-        nc.vector.tensor_copy(v_s[0][:], tab_sc[:, 0, :].indirect(offs_t[:]))
+        nc.vector.memset(v_s[1][:].bitcast(I32), 0)
+        nc.vector.tensor_copy(v_s[0][:], tab_sc[:].indirect(offs_t[:]))
+        for q in range(4):
+            nc.scalar.dma_start(
+                out=v_s[1][32 * q : 32 * q + 4, :].bitcast(I32), in_=v_s[0][32 * q + 4 : 32 * q + 8, :].bitcast(I32)
+            )
+        wn_raw = {(0, 0): load_wn(0, 0, "stage_d")}
         wd_s = sbuf("wd_s", [P, 2, 2, PACK, P], U8)
         nc.vector.tensor_copy(
-            out=wd_s[:].rearrange("p a b t m -> p (a b) m t"),
-            in_=wd_sc_raw[:].rearrange("p a (b m t) -> p (a b) m t", b=2, t=PACK),
+            out=wd_s[:].rearrange("p a b t m -> p (a b) t m"),
+            in_=wd_sc_raw[:].rearrange("p a (b m t) -> p (a b) t m", b=2, t=PACK),
         )
-        wn_raw = {(0, 0): load_wn(0, 0, "stage_c")}
-        gather_words(0, tab_w0)
+        v_w0 = sbuf("v_w0", [P, S], U32, tag="stage_c")
+        nc.vector.tensor_copy(v_w0[:], tab_w0[:].indirect(offs_t[:]))
         wn_raw[1, 0] = load_wn(1, 0, "stage_b")
-        nc.vector.tensor_copy(v_s[1][:], tab_sc[:, 1, :].indirect(offs_t[:]))
-        wn_raw[0, 1] = load_wn(0, 1, "stage_d")
-        gather_words(1, tab_w1)
-        wn_raw[1, 1] = load_wn(1, 1, "stage_a")
+        v_w1 = sbuf("v_w1", [P, S], U32)
+        for f in range(2):
+            nc.vector.tensor_copy(v_w1[:, f * BANK : (f + 1) * BANK], tab_w1[:].indirect(offs_t[:, 32 * f : 32 * (f + 1)]))
+        v_w = [v_w0, v_w1]
+        wn_raw[0, 1] = load_wn(0, 1, "stage_a")
 
         def quantise(name, woven, width):
             codes = sbuf(name + "_w", [P, width], U32)
@@ -130,8 +135,8 @@ def tile_list_newborn_screen_features_kernel(
         def weave_wn(copy, a, b):
             woven = sbuf("wn_woven%d%d" % (a, b), [P, PACK * PASS], BF16, tag="woven", bufs=4)
             copy(
-                woven[:].rearrange("p (t m j) -> p m j t", t=PACK, j=PACK),
-                wn_raw[a, b][:].rearrange("p j (m t) -> p m j t", t=PACK),
+                woven[:].rearrange("p (t m j) -> p m t j", t=PACK, j=PACK),
+                wn_raw[a, b][:].rearrange("p j (m t) -> p m t j", t=PACK),
             )
             return woven
 
@@ -147,11 +152,14 @@ def tile_list_newborn_screen_features_kernel(
         for a in range(2):
             wn_mx[a, 0] = quantise("wn%d0" % a, weave_wn(nc.vector.tensor_copy, a, 0), PASS)
 
-        wb_raw = []
-        for a in range(2):
-            raw = sbuf("wb_raw%d" % a, [P, PACK, N], F32, tag="stage_%s" % "cb"[a])
+        wn_raw[1, 1] = load_wn(1, 1, "stage_d")
+
+        def load_wb(a, tag):
+            raw = sbuf("wb_raw%d" % a, [P, PACK, N], F32, tag=tag)
             nc.sync.dma_start(out=raw[:], in_=wb[a * PASS : (a + 1) * PASS, :].rearrange("(p j) n -> p j n", j=PACK))
-            wb_raw.append(raw)
+            return raw
+
+        wb_raw = [load_wb(0, "stage_b")]
 
         def damping(c):
             b, t = divmod(c, PACK)
@@ -164,7 +172,7 @@ def tile_list_newborn_screen_features_kernel(
                         out=den[:],
                         lhsT=wd_w[:, a, b, t, :].bitcast(FP4X4),
                         lhsT_scale=wd_s[:, a, b, t, :],
-                        rhs=v_w[a][f][:].bitcast(FP8X4),
+                        rhs=v_w[a][:, f * BANK : (f + 1) * BANK].bitcast(FP8X4),
                         rhs_scale=v_s[a][:, f * BANK : (f + 1) * BANK],
                         start=(a == 0),
                         stop=(a == 1),
@@ -188,7 +196,7 @@ def tile_list_newborn_screen_features_kernel(
                         out=num[:],
                         lhsT=codes[:, t * P : (t + 1) * P].bitcast(FP8X4),
                         lhsT_scale=scales[:, t * P : (t + 1) * P],
-                        rhs=v_w[a][f][:].bitcast(FP8X4),
+                        rhs=v_w[a][:, f * BANK : (f + 1) * BANK].bitcast(FP8X4),
                         rhs_scale=v_s[a][:, cols],
                         start=(a == 0),
                         stop=(a == 1),
@@ -202,8 +210,10 @@ def tile_list_newborn_screen_features_kernel(
             b, t = divmod(c, PACK)
             nc.vector.tensor_tensor(dst[:, t, :], h[:].indirect(pos1_t[:]), va_rows[b][:, t, :], ALU.add)
 
-        def pick_b(dst, h, c, offsets):
+        def pick_b(dst, h, offsets):
             nc.vector.tensor_copy(dst, h[:].indirect(offsets))
+
+        def floor_b(dst, c):
             nc.vector.tensor_scalar(out=dst, in0=dst, scalar1=vb_col[:, c : c + 1], scalar2=None, op0=ALU.max)
 
         HALF = PICK // 2
@@ -226,30 +236,33 @@ def tile_list_newborn_screen_features_kernel(
                 damps.append(damping(c + 2))
             if c < 2:
                 wn_mx[c, 1] = quantise("wn%d1" % c, weave_wn(nc.scalar.copy, c, 1), PASS)
-            elif c < 6:
-                quantise_wb(*divmod(c - 2, 2))
+            if c == 0:
+                wb_raw.append(load_wb(1, "stage_a"))
+            for piece in {4: [0], 5: [1, 2, 3]}.get(c, ()):
+                quantise_wb(*divmod(piece, 2))
             if c == PACK:
                 xa_f32.append(sbuf("xa_f32_1", [P, PACK, PICK], F32, tag="slab_a"))
             hs.append(features(c, damps[c]))
+            picked = xb0_f32[:, t, :] if b == 0 else xb10_f32[:, t, :]
+            pick_b(picked, hs[c], pos2_t[:] if b == 0 else pos2_t[:, 0:16])
             pick_a(xa_f32[b], hs[c], c)
-            if b == 0:
-                pick_b(xb0_f32[:, t, :], hs[c], c, pos2_t[:])
-            else:
-                pick_b(xb10_f32[:, t, :], hs[c], c, pos2_t[:, 0:16])
+            floor_b(picked, c)
             if c == PACK - 1:
                 xa_mx = [quantise("xa0", weave(nc.vector.tensor_copy, "xa0", xa_f32[0][:], PICK), PICK)]
                 xb0_mx = quantise("xb0", weave(nc.vector.tensor_copy, "xb0", xb0_f32[:], PICK), PICK)
 
         wa_w = sbuf("wa_w", [P, 2, 2 * N], U8, tag="stage_d")
         nc.sync.dma_start(out=wa_w[:].bitcast(I32), in_=wa_words.rearrange("a p c -> p a c").bitcast(I32))
-        wa_s = sbuf("wa_s", [P, 2, N], U8, tag="stage_a")
+        wa_s = sbuf("wa_s", [P, 2, N], U8, tag="slab_d")
         zero(nc.vector, wa_s)
         load_scale_rows(4 * [nc.sync], wa_s, wa_scales)
-        xa_mx.append(quantise("xa1", weave(nc.scalar.copy, "xa1", xa_f32[1][:], PICK), PICK))
+        xa_mx.append(quantise("xa1", weave(nc.vector.tensor_copy, "xa1", xa_f32[1][:], PICK), PICK))
         xb1_mx = [quantise("xb10", weave(nc.scalar.copy, "xb10", xb10_f32[:], HALF), HALF)]
-        xb11_f32 = sbuf("xb11_f32", [P, PACK, HALF], F32, tag="slab_b")
+        xb11_f32 = sbuf("xb11_f32", [P, PACK, HALF], F32, tag="slab_a")
         for t in range(PACK):
-            pick_b(xb11_f32[:, t, :], hs[PACK + t], PACK + t, pos2_t[:, 16:32])
+            pick_b(xb11_f32[:, t, :], hs[PACK + t], pos2_t[:, 16:32])
+        for t in range(PACK):
+            floor_b(xb11_f32[:, t, :], PACK + t)
         xb1_mx.append(quantise("xb11", weave(nc.vector.tensor_copy, "xb11", xb11_f32[:], HALF), HALF))
 
         ya_sb = []

@@ -1,4 +1,5 @@
 from contextlib import ExitStack
+from functools import partial
 
 import concourse.mybir as mybir
 
@@ -30,10 +31,14 @@ def tile_list_newborn_screen_features_kernel(
     with ExitStack() as ctx:
         lists = ctx.enter_context(tc.tile_pool(name="lists", bufs=1))
         keep = ctx.enter_context(tc.tile_pool(name="keep", bufs=1))
+        stage = ctx.enter_context(tc.tile_pool(name="stage", bufs=1))
         psum = ctx.enter_context(tc.psum_pool(name="psum", bufs=4))
 
         def sbuf(name, shape, dtype, tag=None, bufs=1):
             return keep.tile(shape, dtype, name=name, tag=tag or name, bufs=bufs, align_bytes=ALIGN)
+
+        def staged(name, shape, dtype, kib):
+            return stage.tile(shape, dtype, name=name, align_bytes=ALIGN, offset=1024 * kib)
 
         def load_scale_rows(engines, plane, scales):
             for q, engine in enumerate(engines):
@@ -45,27 +50,33 @@ def tile_list_newborn_screen_features_kernel(
         def zero(engine, plane):
             engine.memset(plane[:].rearrange("p a c -> p (a c)").bitcast(I32), 0)
 
+        warm = sbuf("warm", [P, 2], F32)
+        nc.gpsimd.memset(warm[:, 0:1], 1.0)
+        nc.scalar.activation(out=warm[:, 1:2], in_=warm[:, 0:1], func=ACT.Abs_reciprocal_sqrt)
+
         offs_t = lists.tile([P, S // 16], U16, name="offs_t")
         pos1_t = lists.tile([P, PICK // 16], U16, name="pos1_t")
         pos2_t = lists.tile([P, PICK // 16], U16, name="pos2_t")
         nc.sync.dma_start(offs_t[:], offs)
         nc.sync.dma_start(pos1_t[:], pos1)
         nc.sync.dma_start(pos2_t[:], pos2)
+        wd_raw = staged("wd_raw", [P, 2, 2 * H], U8, 16)
+        nc.sync.dma_start(out=wd_raw[:].bitcast(I32), in_=wd_words.rearrange("a p c -> p a c").bitcast(I32))
 
-        tab_sc = sbuf("tab_sc", [P, T], U8, tag="stage_d")
+        wd_sc_raw = staged("wd_sc_raw", [P, 2, H], U8, 48)
+        zero(nc.gpsimd, wd_sc_raw)
+        load_scale_rows(2 * [nc.gpsimd] + 2 * [nc.scalar], wd_sc_raw, wd_scales)
+        tab_sc = staged("tab_sc", [P, T], U8, 38)
         nc.vector.memset(tab_sc[:].bitcast(I32), 0)
         for q in range(4):
             nc.scalar.dma_start(
                 out=tab_sc[32 * q : 32 * q + 8, :].bitcast(I32), in_=tab_scales[:, 4 * q : 4 * q + 4, :].bitcast(I32)
             )
 
-        wd_sc_raw = sbuf("wd_sc_raw", [P, 2, H], U8, tag="stage_c")
-        zero(nc.vector, wd_sc_raw)
-        load_scale_rows(2 * [nc.gpsimd] + 2 * [nc.scalar], wd_sc_raw, wd_scales)
 
         def load_channel_vector(name, vec):
             col = sbuf(name, [P, 2 * PACK], F32)
-            nc.gpsimd.dma_start(
+            nc.scalar.dma_start(
                 out=col[:].rearrange("p (b t) -> p b t", b=2), in_=vec.rearrange("(b p t) -> p b t", b=2, t=PACK)
             )
             return col
@@ -74,21 +85,22 @@ def tile_list_newborn_screen_features_kernel(
         gain_col = load_channel_vector("gain_col", gain)
         vb_col = load_channel_vector("vb_col", vb)
 
-        wd_raw = sbuf("wd_raw", [P, 2, 2 * H], U8, tag="stage_a")
-        nc.sync.dma_start(out=wd_raw[:].bitcast(I32), in_=wd_words.rearrange("a p c -> p a c").bitcast(I32))
 
-        def load_tab(a, tag):
-            words = sbuf("tab_w%d" % a, [P, T], U32, tag=tag)
+        def load_tab(a):
+            words = staged("tab_w%d" % a, [P, T], U32, 16 * a)
             nc.sync.dma_start(out=words[:].bitcast(I32), in_=tab_words[a].rearrange("p t i -> p (t i)").bitcast(I32))
             return words
 
-        def load_wn(a, b, tag):
-            raw = sbuf("wn_raw%d%d" % (a, b), [P, PACK, PASS], F32, tag=tag)
-            rows = wn[a * PASS : (a + 1) * PASS, b * PASS : (b + 1) * PASS]
-            nc.sync.dma_start(out=raw[:], in_=rows.rearrange("(p j) c -> p j c", j=PACK))
+        def load_wn(a, b):
+            pieces = 2 if (a, b) == (1, 0) else 1
+            width = PASS // pieces
+            raw = staged("wn_raw%d%d" % (a, b), [P, pieces, PACK, width], F32, 8 * a + (0 if b else 32))
+            for g in range(pieces):
+                rows = wn[a * PASS : (a + 1) * PASS, b * PASS + g * width : b * PASS + (g + 1) * width]
+                nc.sync.dma_start(out=raw[:, g, :, :], in_=rows.rearrange("(p j) c -> p j c", j=PACK))
             return raw
 
-        tab_w0 = load_tab(0, "stage_b")
+        tab_w0 = load_tab(0)
 
         va_rows = []
         for b in range(2):
@@ -103,41 +115,44 @@ def tile_list_newborn_screen_features_kernel(
             out=wd_w[:].bitcast(U16).rearrange("p a b t m -> p (a b) t m"),
             in_=wd_raw[:].bitcast(U16).rearrange("p a (b m t) -> p (a b) t m", b=2, t=PACK),
         )
-        tab_w1 = load_tab(1, "stage_a")
-        v_s = [sbuf("v_s%d" % a, [P, S], U8) for a in range(2)]
-        nc.vector.memset(v_s[1][:].bitcast(I32), 0)
-        nc.vector.tensor_copy(v_s[0][:], tab_sc[:].indirect(offs_t[:]))
-        for q in range(4):
-            nc.scalar.dma_start(
-                out=v_s[1][32 * q : 32 * q + 4, :].bitcast(I32), in_=v_s[0][32 * q + 4 : 32 * q + 8, :].bitcast(I32)
-            )
-        wn_raw = {(0, 0): load_wn(0, 0, "stage_d")}
+        tab_w1 = load_tab(1)
         wd_s = sbuf("wd_s", [P, 2, 2, PACK, P], U8)
         nc.vector.tensor_copy(
             out=wd_s[:].rearrange("p a b t m -> p (a b) t m"),
             in_=wd_sc_raw[:].rearrange("p a (b m t) -> p (a b) t m", b=2, t=PACK),
         )
-        v_w0 = sbuf("v_w0", [P, S], U32, tag="stage_c")
+        v_s = [staged("v_s0", [P, S], U8, 48), sbuf("v_s1", [P, S], U8)]
+        nc.vector.memset(v_s[1][:].bitcast(I32), 0)
+        nc.vector.tensor_copy(v_s[0][:], tab_sc[:].indirect(offs_t[:]))
+        for q in range(4):
+            nc.sync.dma_start(
+                out=v_s[1][32 * q : 32 * q + 4, :].bitcast(I32), in_=v_s[0][32 * q + 4 : 32 * q + 8, :].bitcast(I32)
+            )
+        wn_raw = {(a, 0): load_wn(a, 0) for a in range(2)}
+        v_w0 = staged("v_w0", [P, S], U32, 49)
         nc.vector.tensor_copy(v_w0[:], tab_w0[:].indirect(offs_t[:]))
-        wn_raw[1, 0] = load_wn(1, 0, "stage_b")
+        for a in range(2):
+            wn_raw[a, 1] = load_wn(a, 1)
         v_w1 = sbuf("v_w1", [P, S], U32)
         for f in range(2):
             nc.vector.tensor_copy(v_w1[:, f * BANK : (f + 1) * BANK], tab_w1[:].indirect(offs_t[:, 32 * f : 32 * (f + 1)]))
         v_w = [v_w0, v_w1]
-        wn_raw[0, 1] = load_wn(0, 1, "stage_a")
 
-        def quantise(name, woven, width):
+        def quantise(name, woven, width, first=0):
             codes = sbuf(name + "_w", [P, width], U32)
             scales = sbuf(name + "_s", [P, width], U8)
-            nc.vector.quantize_mx(out=codes[:].bitcast(FP8X4), scales=scales[:], in_=woven[:])
+            for lo, hi in ((0, first), (first, width)) if first else ((0, width),):
+                nc.vector.quantize_mx(
+                    out=codes[:, lo:hi].bitcast(FP8X4), scales=scales[:, lo:hi], in_=woven[:, PACK * lo : PACK * hi]
+                )
             return codes, scales
 
         def weave_wn(copy, a, b):
             woven = sbuf("wn_woven%d%d" % (a, b), [P, PACK * PASS], BF16, tag="woven", bufs=4)
-            copy(
-                woven[:].rearrange("p (t m j) -> p m t j", t=PACK, j=PACK),
-                wn_raw[a, b][:].rearrange("p j (m t) -> p m t j", t=PACK),
-            )
+            pieces = wn_raw[a, b].shape[1]
+            dealt = woven[:].rearrange("p (t g m j) -> p g m t j", t=PACK, g=pieces, j=PACK)
+            for g in range(pieces):
+                copy(dealt[:, g], wn_raw[a, b][:, g].rearrange("p j (m t) -> p m t j", t=PACK))
             return woven
 
         def weave(copy, name, planes, width):
@@ -150,20 +165,22 @@ def tile_list_newborn_screen_features_kernel(
 
         wn_mx = {}
         for a in range(2):
-            wn_mx[a, 0] = quantise("wn%d0" % a, weave_wn(nc.vector.tensor_copy, a, 0), PASS)
+            wn_mx[a, 0] = quantise("wn%d0" % a, weave_wn(nc.vector.tensor_copy, a, 0), PASS, first=P * a)
 
-        wn_raw[1, 1] = load_wn(1, 1, "stage_d")
 
-        def load_wb(a, tag):
-            raw = sbuf("wb_raw%d" % a, [P, PACK, N], F32, tag=tag)
+        def load_wb(a):
+            raw = staged("wb_raw%d" % a, [P, PACK, N], F32, 16 + 16 * a)
             nc.sync.dma_start(out=raw[:], in_=wb[a * PASS : (a + 1) * PASS, :].rearrange("(p j) n -> p j n", j=PACK))
             return raw
 
-        wb_raw = [load_wb(0, "stage_b")]
+        wb_raw = [load_wb(a) for a in range(2)]
+
+        scratch = sbuf("scratch", [P, (2 * PACK + 1) * S], F32)
+        scratch_rows = scratch[:].rearrange("p (c s) -> p c s", s=S)
 
         def damping(c):
             b, t = divmod(c, PACK)
-            damp = sbuf("damp%d" % c, [P, S], F32, tag="damp", bufs=8)
+            damp = scratch[:, c * S : (c + 1) * S]
             halves = [damp[:, f * BANK : (f + 1) * BANK] for f in range(2)]
             for f in range(2):
                 den = psum.tile([P, BANK], F32, name="den%d%d" % (c, f), tag="left")
@@ -213,8 +230,8 @@ def tile_list_newborn_screen_features_kernel(
         def pick_b(dst, h, offsets):
             nc.vector.tensor_copy(dst, h[:].indirect(offsets))
 
-        def floor_b(dst, c):
-            nc.vector.tensor_scalar(out=dst, in0=dst, scalar1=vb_col[:, c : c + 1], scalar2=None, op0=ALU.max)
+        def floor_b(dst, src, c):
+            nc.vector.tensor_scalar(out=dst, in0=src, scalar1=vb_col[:, c : c + 1], scalar2=None, op0=ALU.max)
 
         HALF = PICK // 2
         xa_f32 = [sbuf("xa_f32_0", [P, PACK, PICK], F32, tag="slab_d")]
@@ -236,41 +253,42 @@ def tile_list_newborn_screen_features_kernel(
                 damps.append(damping(c + 2))
             if c < 2:
                 wn_mx[c, 1] = quantise("wn%d1" % c, weave_wn(nc.scalar.copy, c, 1), PASS)
-            if c == 0:
-                wb_raw.append(load_wb(1, "stage_a"))
-            for piece in {4: [0], 5: [1, 2, 3]}.get(c, ()):
+            for piece in {5: [0, 1, 2, 3]}.get(c, ()):
                 quantise_wb(*divmod(piece, 2))
             if c == PACK:
                 xa_f32.append(sbuf("xa_f32_1", [P, PACK, PICK], F32, tag="slab_a"))
             hs.append(features(c, damps[c]))
+            if c > 0:
+                floor_previous()
+            if c == PACK:
+                xb0_mx = quantise("xb0", weave(nc.scalar.copy, "xb0", scratch_rows[:, 1 : PACK + 1, 0:PICK], PICK), PICK)
             picked = xb0_f32[:, t, :] if b == 0 else xb10_f32[:, t, :]
             pick_b(picked, hs[c], pos2_t[:] if b == 0 else pos2_t[:, 0:16])
             pick_a(xa_f32[b], hs[c], c)
-            floor_b(picked, c)
+            floor_previous = partial(floor_b, scratch_rows[:, c + 1, 0 : (PICK if b == 0 else HALF)], picked, c)
             if c == PACK - 1:
                 xa_mx = [quantise("xa0", weave(nc.vector.tensor_copy, "xa0", xa_f32[0][:], PICK), PICK)]
-                xb0_mx = quantise("xb0", weave(nc.vector.tensor_copy, "xb0", xb0_f32[:], PICK), PICK)
+        floor_previous()
 
-        wa_w = sbuf("wa_w", [P, 2, 2 * N], U8, tag="stage_d")
+        wa_w = staged("wa_w", [P, 2, 2 * N], U8, 44)
         nc.sync.dma_start(out=wa_w[:].bitcast(I32), in_=wa_words.rearrange("a p c -> p a c").bitcast(I32))
-        wa_s = sbuf("wa_s", [P, 2, N], U8, tag="slab_d")
-        zero(nc.vector, wa_s)
+        wa_s = wd_s[:].rearrange("p a b t m -> p a (b t m)")[:, :, 0:N]
         load_scale_rows(4 * [nc.sync], wa_s, wa_scales)
         xa_mx.append(quantise("xa1", weave(nc.vector.tensor_copy, "xa1", xa_f32[1][:], PICK), PICK))
-        xb1_mx = [quantise("xb10", weave(nc.scalar.copy, "xb10", xb10_f32[:], HALF), HALF)]
+        xb1_mx = [quantise("xb10", weave(nc.scalar.copy, "xb10", scratch_rows[:, PACK + 1 :, 0:HALF], HALF), HALF)]
         xb11_f32 = sbuf("xb11_f32", [P, PACK, HALF], F32, tag="slab_a")
         for t in range(PACK):
             pick_b(xb11_f32[:, t, :], hs[PACK + t], pos2_t[:, 16:32])
         for t in range(PACK):
-            floor_b(xb11_f32[:, t, :], PACK + t)
+            floor_b(xb11_f32[:, t, :], xb11_f32[:, t, :], PACK + t)
         xb1_mx.append(quantise("xb11", weave(nc.vector.tensor_copy, "xb11", xb11_f32[:], HALF), HALF))
 
         ya_sb = []
         for pair in range(N // (2 * P)):
-            ya = sbuf("ya%d" % pair, [P, 2, PICK], F32, tag="damp", bufs=8)
+            ya = scratch_rows[:, pair, :].rearrange("p (i j) -> p i j", i=2)
             for i in range(2):
                 n = 2 * pair + i
-                acc = psum.tile([P, PICK], F32, name="ya_acc%d" % n, tag="left")
+                acc = psum.tile([P, PICK], F32, name="ya_acc%d" % n, tag="left" if n < 4 else "right")
                 for a in range(2):
                     codes, scales = xa_mx[a]
                     nc.tensor.matmul_mx(
@@ -290,10 +308,10 @@ def tile_list_newborn_screen_features_kernel(
             cols = slice(f * HALF, (f + 1) * HALF)
             moving = [(xb0_mx[0][:, cols], xb0_mx[1][:, cols]), (xb1_mx[f][0][:], xb1_mx[f][1][:])]
             for pair in range(N // (2 * P)):
-                acc = psum.tile([P, 2, HALF], F32, name="yb_acc%d%d" % (f, pair), tag="right")
-                for i in range(2):
-                    g, n = divmod(2 * pair + i, N // (2 * P))
-                    for a in range(2):
+                acc = psum.tile([P, 2, HALF], F32, name="yb_acc%d%d" % (f, pair), tag="right" if 3 * f + pair < 2 else "left")
+                for a in range(2):
+                    for i in range(2):
+                        g, n = divmod(2 * pair + i, N // (2 * P))
                         codes, scales = wb_mx[a, g]
                         nc.tensor.matmul_mx(
                             out=acc[:, i, :],
@@ -301,8 +319,8 @@ def tile_list_newborn_screen_features_kernel(
                             lhsT_scale=scales[:, n * P : (n + 1) * P],
                             rhs=moving[a][0].bitcast(FP8X4),
                             rhs_scale=moving[a][1],
-                            start=(a == 0),
-                            stop=(a == 1),
+                            start=(a == 0 and i == 0),
+                            stop=(a == 1 and i == 1),
                         )
                 result = ya_sb[pair][:, :, cols]
                 nc.vector.tensor_tensor(out=result, in0=acc[:], in1=result, op=ALU.min)

from contextlib import ExitStack
from functools import partial

import concourse.mybir as mybir

K, H, N, T, S, PICK = 1024, 1024, 768, 4096, 1024, 512
FLOPS = 2 * (2 * K * H * S + 2 * H * N * PICK)

F32 = mybir.dt.float32
BF16 = mybir.dt.bfloat16
I32 = mybir.dt.int32
U32 = mybir.dt.uint32
U16 = mybir.dt.uint16
U8 = mybir.dt.uint8
FP8X4 = mybir.dt.float8_e4m3fn_x4
FP4X4 = mybir.dt.float4_e2m1fn_x4
ALU = mybir.AluOpType
ACT = mybir.ActivationFunctionType

P = 128
PACK = 4
PASS = P * PACK
BANK = 512
ALIGN = 64


def tile_list_newborn_screen_features_kernel(
    tc, tab_words, tab_scales, offs, pos1, pos2, wn, wd_words, wd_scales, gain, va, vb, wa_words, wa_scales, wb, out
):
    nc = tc.nc
    with ExitStack() as ctx:
        lists = ctx.enter_context(tc.tile_pool(name="lists", bufs=1))
        keep = ctx.enter_context(tc.tile_pool(name="keep", bufs=1))
        stage = ctx.enter_context(tc.tile_pool(name="stage", bufs=1))
        psum = ctx.enter_context(tc.psum_pool(name="psum", bufs=4))

        def sbuf(name, shape, dtype, tag=None, bufs=1):
            return keep.tile(shape, dtype, name=name, tag=tag or name, bufs=bufs, align_bytes=ALIGN)

        def staged(name, shape, dtype, kib):
            return stage.tile(shape, dtype, name=name, align_bytes=ALIGN, offset=1024 * kib)

        def load_scale_rows(engines, plane, scales):
            for q, engine in enumerate(engines):
                engine.dma_start(
                    out=plane[32 * q : 32 * q + 4, :, :].bitcast(I32),
                    in_=scales[:, 4 * q : 4 * q + 4, :].rearrange("a r c -> r a c").bitcast(I32),
                )

        def zero(engine, plane):
            engine.memset(plane[:].rearrange("p a c -> p (a c)").bitcast(I32), 0)

        warm = sbuf("warm", [P, 2], F32)
        nc.gpsimd.memset(warm[:, 0:1], 1.0)
        nc.scalar.activation(out=warm[:, 1:2], in_=warm[:, 0:1], func=ACT.Abs_reciprocal_sqrt)

        offs_t = lists.tile([P, S // 16], U16, name="offs_t")
        pos1_t = lists.tile([P, PICK // 16], U16, name="pos1_t")
        pos2_t = lists.tile([P, PICK // 16], U16, name="pos2_t")
        nc.sync.dma_start(offs_t[:], offs)
        nc.sync.dma_start(pos1_t[:], pos1)
        nc.sync.dma_start(pos2_t[:], pos2)
        wd_raw = staged("wd_raw", [P, 2, 2 * H], U8, 16)
        nc.sync.dma_start(out=wd_raw[:].bitcast(I32), in_=wd_words.rearrange("a p c -> p a c").bitcast(I32))

        wd_sc_raw = staged("wd_sc_raw", [P, 2, H], U8, 48)
        zero(nc.gpsimd, wd_sc_raw)
        load_scale_rows(2 * [nc.gpsimd] + 2 * [nc.scalar], wd_sc_raw, wd_scales)
        tab_sc = staged("tab_sc", [P, T], U8, 38)
        nc.vector.memset(tab_sc[:].bitcast(I32), 0)
        for q in range(4):
            nc.scalar.dma_start(
                out=tab_sc[32 * q : 32 * q + 8, :].bitcast(I32), in_=tab_scales[:, 4 * q : 4 * q + 4, :].bitcast(I32)
            )


        def load_channel_vector(name, vec):
            col = sbuf(name, [P, 2 * PACK], F32)
            nc.scalar.dma_start(
                out=col[:].rearrange("p (b t) -> p b t", b=2), in_=vec.rearrange("(b p t) -> p b t", b=2, t=PACK)
            )
            return col

        va_col = load_channel_vector("va_col", va)
        gain_col = load_channel_vector("gain_col", gain)
        vb_col = load_channel_vector("vb_col", vb)


        def load_tab(a):
            words = staged("tab_w%d" % a, [P, T], U32, 16 * a)
            nc.sync.dma_start(out=words[:].bitcast(I32), in_=tab_words[a].rearrange("p t i -> p (t i)").bitcast(I32))
            return words

        def load_wn(a, b):
            pieces = 2 if (a, b) == (1, 0) else 1
            width = PASS // pieces
            raw = staged("wn_raw%d%d" % (a, b), [P, pieces, PACK, width], F32, 8 * a + (0 if b else 32))
            for g in range(pieces):
                rows = wn[a * PASS : (a + 1) * PASS, b * PASS + g * width : b * PASS + (g + 1) * width]
                nc.sync.dma_start(out=raw[:, g, :, :], in_=rows.rearrange("(p j) c -> p j c", j=PACK))
            return raw

        tab_w0 = load_tab(0)

        va_rows = []
        for b in range(2):
            rows = sbuf("va_rows%d" % b, [P, PACK, PICK], F32, tag="slab_%s" % "ab"[b])
            for t in range(PACK):
                c = PACK * b + t
                nc.scalar.copy(out=rows[:, t, :], in_=va_col[:, c : c + 1].to_broadcast([P, PICK]))
            va_rows.append(rows)

        wd_w = sbuf("wd_w", [P, 2, 2, PACK, 2 * P], U8)
        nc.vector.tensor_copy(
            out=wd_w[:].bitcast(U16).rearrange("p a b t m -> p (a b) t m"),
            in_=wd_raw[:].bitcast(U16).rearrange("p a (b m t) -> p (a b) t m", b=2, t=PACK),
        )
        tab_w1 = load_tab(1)
        wd_s = sbuf("wd_s", [P, 2, 2, PACK, P], U8)
        nc.vector.tensor_copy(
            out=wd_s[:].rearrange("p a b t m -> p (a b) t m"),
            in_=wd_sc_raw[:].rearrange("p a (b m t) -> p (a b) t m", b=2, t=PACK),
        )
        v_s = [staged("v_s0", [P, S], U8, 48), sbuf("v_s1", [P, S], U8)]
        nc.vector.memset(v_s[1][:].bitcast(I32), 0)
        nc.vector.tensor_copy(v_s[0][:], tab_sc[:].indirect(offs_t[:]))
        for q in range(4):
            nc.sync.dma_start(
                out=v_s[1][32 * q : 32 * q + 4, :].bitcast(I32), in_=v_s[0][32 * q + 4 : 32 * q + 8, :].bitcast(I32)
            )
        wn_raw = {(a, 0): load_wn(a, 0) for a in range(2)}
        v_w0 = staged("v_w0", [P, S], U32, 49)
        nc.vector.tensor_copy(v_w0[:], tab_w0[:].indirect(offs_t[:]))
        for a in range(2):
            wn_raw[a, 1] = load_wn(a, 1)
        v_w1 = sbuf("v_w1", [P, S], U32)
        for f in range(2):
            nc.vector.tensor_copy(v_w1[:, f * BANK : (f + 1) * BANK], tab_w1[:].indirect(offs_t[:, 32 * f : 32 * (f + 1)]))
        v_w = [v_w0, v_w1]

        def quantise(name, woven, width, first=0):
            codes = sbuf(name + "_w", [P, width], U32)
            scales = sbuf(name + "_s", [P, width], U8)
            for lo, hi in ((0, first), (first, width)) if first else ((0, width),):
                nc.vector.quantize_mx(
                    out=codes[:, lo:hi].bitcast(FP8X4), scales=scales[:, lo:hi], in_=woven[:, PACK * lo : PACK * hi]
                )
            return codes, scales

        def weave_wn(copy, a, b):
            woven = sbuf("wn_woven%d%d" % (a, b), [P, PACK * PASS], BF16, tag="woven", bufs=4)
            pieces = wn_raw[a, b].shape[1]
            dealt = woven[:].rearrange("p (t g m j) -> p g m t j", t=PACK, g=pieces, j=PACK)
            for g in range(pieces):
                copy(dealt[:, g], wn_raw[a, b][:, g].rearrange("p j (m t) -> p m t j", t=PACK))
            return woven

        def weave(copy, name, planes, width):
            woven = sbuf(name + "_woven", [P, PACK * width], BF16, tag="woven", bufs=4)
            copy(
                woven[:].rearrange("p (c i t) -> p c t i", i=4, t=PACK),
                planes.rearrange("p t (c i) -> p c t i", i=4),
            )
            return woven

        wn_mx = {}
        for a in range(2):
            wn_mx[a, 0] = quantise("wn%d0" % a, weave_wn(nc.vector.tensor_copy, a, 0), PASS, first=P * a)


        def load_wb(a):
            raw = staged("wb_raw%d" % a, [P, PACK, N], F32, 16 + 16 * a)
            nc.sync.dma_start(out=raw[:], in_=wb[a * PASS : (a + 1) * PASS, :].rearrange("(p j) n -> p j n", j=PACK))
            return raw

        wb_raw = [load_wb(a) for a in range(2)]

        scratch = sbuf("scratch", [P, (2 * PACK + 1) * S], F32)
        scratch_rows = scratch[:].rearrange("p (c s) -> p c s", s=S)

        def damping(c):
            b, t = divmod(c, PACK)
            damp = scratch[:, c * S : (c + 1) * S]
            halves = [damp[:, f * BANK : (f + 1) * BANK] for f in range(2)]
            for f in range(2):
                den = psum.tile([P, BANK], F32, name="den%d%d" % (c, f), tag="left")
                for a in range(2):
                    nc.tensor.matmul_mx(
                        out=den[:],
                        lhsT=wd_w[:, a, b, t, :].bitcast(FP4X4),
                        lhsT_scale=wd_s[:, a, b, t, :],
                        rhs=v_w[a][:, f * BANK : (f + 1) * BANK].bitcast(FP8X4),
                        rhs_scale=v_s[a][:, f * BANK : (f + 1) * BANK],
                        start=(a == 0),
                        stop=(a == 1),
                    )
                nc.scalar.activation(out=halves[f], in_=den[:], func=ACT.Abs)
            for half in halves:
                nc.scalar.activation(out=half, in_=half, func=ACT.Abs_reciprocal_sqrt, bias=1.0)
            for half in halves:
                nc.scalar.activation(out=half, in_=half, func=ACT.Square)
            return damp

        def features(c, damp):
            b, t = divmod(c, PACK)
            h = sbuf("h%d" % c, [P, S], F32, tag="h", bufs=6)
            for f in range(2):
                cols = slice(f * BANK, (f + 1) * BANK)
                num = psum.tile([P, BANK], F32, name="num%d%d" % (c, f), tag="right")
                for a in range(2):
                    codes, scales = wn_mx[a, b]
                    nc.tensor.matmul_mx(
                        out=num[:],
                        lhsT=codes[:, t * P : (t + 1) * P].bitcast(FP8X4),
                        lhsT_scale=scales[:, t * P : (t + 1) * P],
                        rhs=v_w[a][:, f * BANK : (f + 1) * BANK].bitcast(FP8X4),
                        rhs_scale=v_s[a][:, cols],
                        start=(a == 0),
                        stop=(a == 1),
                    )
                nc.vector.scalar_tensor_tensor(
                    out=h[:, cols], in0=num[:], scalar=gain_col[:, c : c + 1], in1=damp[:, cols], op0=ALU.mult, op1=ALU.mult
                )
            return h

        def pick_a(dst, h, c):
            b, t = divmod(c, PACK)
            nc.vector.tensor_tensor(dst[:, t, :], h[:].indirect(pos1_t[:]), va_rows[b][:, t, :], ALU.add)

        def pick_b(dst, h, offsets):
            nc.vector.tensor_copy(dst, h[:].indirect(offsets))

        def floor_b(dst, src, c):
            nc.vector.tensor_scalar(out=dst, in0=src, scalar1=vb_col[:, c : c + 1], scalar2=None, op0=ALU.max)

        HALF = PICK // 2
        xa_f32 = [sbuf("xa_f32_0", [P, PACK, PICK], F32, tag="slab_d")]
        xb0_f32 = sbuf("xb0_f32", [P, PACK, PICK], F32)
        xb10_f32 = sbuf("xb10_f32", [P, PACK, HALF], F32)
        damps = [damping(0), damping(1)]
        hs = []
        wn_woven = {}
        wb_mx = {}

        def quantise_wb(a, g):
            name = "wb%d%d" % (a, g)
            planes = wb_raw[a][:, :, g * (N // 2) : (g + 1) * (N // 2)]
            wb_mx[a, g] = quantise(name, weave(nc.scalar.copy, name, planes, N // 2), N // 2)

        for c in range(2 * PACK):
            b, t = divmod(c, PACK)
            if c + 2 < 2 * PACK:
                damps.append(damping(c + 2))
            if c < 2:
                wn_mx[c, 1] = quantise("wn%d1" % c, weave_wn(nc.scalar.copy, c, 1), PASS)
            for piece in {5: [0, 1, 2, 3]}.get(c, ()):
                quantise_wb(*divmod(piece, 2))
            if c == PACK:
                xa_f32.append(sbuf("xa_f32_1", [P, PACK, PICK], F32, tag="slab_a"))
            hs.append(features(c, damps[c]))
            if c > 0:
                floor_previous()
            if c == PACK:
                xb0_mx = quantise("xb0", weave(nc.scalar.copy, "xb0", scratch_rows[:, 1 : PACK + 1, 0:PICK], PICK), PICK)
            picked = xb0_f32[:, t, :] if b == 0 else xb10_f32[:, t, :]
            pick_b(picked, hs[c], pos2_t[:] if b == 0 else pos2_t[:, 0:16])
            pick_a(xa_f32[b], hs[c], c)
            floor_previous = partial(floor_b, scratch_rows[:, c + 1, 0 : (PICK if b == 0 else HALF)], picked, c)
            if c == PACK - 1:
                xa_mx = [quantise("xa0", weave(nc.vector.tensor_copy, "xa0", xa_f32[0][:], PICK), PICK)]
        floor_previous()

        wa_w = staged("wa_w", [P, 2, 2 * N], U8, 44)
        nc.sync.dma_start(out=wa_w[:].bitcast(I32), in_=wa_words.rearrange("a p c -> p a c").bitcast(I32))
        wa_s = wd_s[:].rearrange("p a b t m -> p a (b t m)")[:, :, 0:N]
        load_scale_rows(4 * [nc.sync], wa_s, wa_scales)
        xa_mx.append(quantise("xa1", weave(nc.vector.tensor_copy, "xa1", xa_f32[1][:], PICK), PICK))
        xb1_mx = [quantise("xb10", weave(nc.scalar.copy, "xb10", scratch_rows[:, PACK + 1 :, 0:HALF], HALF), HALF)]
        xb11_f32 = sbuf("xb11_f32", [P, PACK, HALF], F32, tag="slab_a")
        for t in range(PACK):
            pick_b(xb11_f32[:, t, :], hs[PACK + t], pos2_t[:, 16:32])
        for t in range(PACK):
            floor_b(xb11_f32[:, t, :], xb11_f32[:, t, :], PACK + t)
        xb1_mx.append(quantise("xb11", weave(nc.vector.tensor_copy, "xb11", xb11_f32[:], HALF), HALF))

        ya_sb = []
        for pair in range(N // (2 * P)):
            ya = scratch_rows[:, pair, :].rearrange("p (i j) -> p i j", i=2)
            for i in range(2):
                n = 2 * pair + i
                acc = psum.tile([P, PICK], F32, name="ya_acc%d" % n, tag="left" if n < 4 else "right")
                for a in range(2):
                    codes, scales = xa_mx[a]
                    nc.tensor.matmul_mx(
                        out=acc[:],
                        lhsT=wa_w[:, a, 2 * n * P : 2 * (n + 1) * P].bitcast(FP4X4),
                        lhsT_scale=wa_s[:, a, n * P : (n + 1) * P],
                        rhs=codes[:].bitcast(FP8X4),
                        rhs_scale=scales[:],
                        start=(a == 0),
                        stop=(a == 1),
                    )
                nc.scalar.copy(out=ya[:, i, :], in_=acc[:])
            ya_sb.append(ya)

        out_rows = out.rearrange("(g p) j -> p g j", p=P)
        for f in range(2):
            cols = slice(f * HALF, (f + 1) * HALF)
            moving = [(xb0_mx[0][:, cols], xb0_mx[1][:, cols]), (xb1_mx[f][0][:], xb1_mx[f][1][:])]
            for pair in range(N // (2 * P)):
                acc = psum.tile([P, 2, HALF], F32, name="yb_acc%d%d" % (f, pair), tag="right" if 3 * f + pair < 2 else "left")
                for a in range(2):
                    for i in range(2):
                        g, n = divmod(2 * pair + i, N // (2 * P))
                        codes, scales = wb_mx[a, g]
                        nc.tensor.matmul_mx(
                            out=acc[:, i, :],
                            lhsT=codes[:, n * P : (n + 1) * P].bitcast(FP8X4),
                            lhsT_scale=scales[:, n * P : (n + 1) * P],
                            rhs=moving[a][0].bitcast(FP8X4),
                            rhs_scale=moving[a][1],
                            start=(a == 0 and i == 0),
                            stop=(a == 1 and i == 1),
                        )
                result = ya_sb[pair][:, :, cols]
                nc.vector.tensor_tensor(out=result, in0=acc[:], in1=result, op=ALU.min)
                nc.sync.dma_start(out=out_rows[:, 2 * pair : 2 * pair + 2, cols], in_=result)
